import numpy as np
import ml_dtypes


def mxq(x, axis, fmt="e4m3"):
    dtype, down = {"e4m3": (ml_dtypes.float8_e4m3fn, 7), "e5m2": (ml_dtypes.float8_e5m2, 14)}[fmt]
    v = np.moveaxis(np.asarray(x, np.float32).astype(ml_dtypes.bfloat16).astype(np.float64), axis, -1)
    blocks = v.reshape(v.shape[:-1] + (-1, 32))
    amax = np.abs(blocks).max(-1, keepdims=True)
    byte = np.maximum(np.where(amax > 0, np.frexp(amax)[1] - 1 + 127, 0) - down, 1)
    scale = np.exp2(byte - 127.0)
    codes = (blocks / scale).astype(np.float32).astype(dtype).astype(np.float64)
    return np.moveaxis((codes * scale).reshape(v.shape), -1, axis)


WIDE = False


def mx_kscale(k):
    if not WIDE:
        return np.ones(k)
    levels = np.array([10, -10, 5, -5, 0])
    if k % 512:
        return np.exp2(np.random.permutation(np.resize(levels, k // 32))).repeat(32)
    a = np.empty((k // 512, 16))
    for p in range(k // 512):
        a[p, :8] = np.random.permutation(np.resize(levels, 8))
        for g in range(8):
            far = levels[np.abs(levels - a[p, g]) >= 10]
            a[p, g + 8] = far[np.random.randint(len(far))]
    return np.exp2(a.ravel()).repeat(32)


def f64(x):
    return np.asarray(x).astype(np.float64)


def striped(idx):
    return np.tile(np.asarray(idx).reshape(-1, 16).T, (8, 1)).astype(np.uint16)


def unstriped(offs):
    return offs[:16].T.reshape(-1).astype(np.int64)


E2M1 = np.array([0.0, 0.5, 1.0, 1.5, 2.0, 3.0, 4.0, 6.0, -0.0, -0.5, -1.0, -1.5, -2.0, -3.0, -4.0, -6.0])


def pack_weight(w, fmt):
    k, n = w.shape
    w = f64(np.asarray(w, np.float32).astype(ml_dtypes.bfloat16)).reshape(k // 32, 32, n)
    amax = np.abs(w).max(1)
    if fmt == "e4m3":
        byte = np.frexp(amax)[1] - 1 + 127 - 7
    else:
        mant, ex = np.frexp(amax / 6.0)
        byte = np.where(mant > 0.5, ex, ex - 1) + 127
    byte = np.clip(np.where(amax > 0, byte, 1), 1, 254)
    scaled = (w * np.exp2(127.0 - byte)[:, None, :]).reshape(k, n).astype(np.float32)
    by_word = np.ascontiguousarray(scaled.reshape(k // 512, 128, 4, n).transpose(0, 1, 3, 2))
    if fmt == "e4m3":
        words = by_word.astype(ml_dtypes.float8_e4m3fn).view(np.uint8)
    else:
        c = by_word.astype(ml_dtypes.float4_e2m1fn).view(np.uint8) & 0xF
        words = (c[..., 0::2] | (c[..., 1::2] << 4)).reshape(k // 512, 128, 2 * n)
    return np.ascontiguousarray(words), np.ascontiguousarray(byte.astype(np.uint8).reshape(k // 512, 16, n))


def unpack_weight(words, scales, fmt):
    g, _, n = scales.shape
    words = np.ascontiguousarray(words).reshape(g, 128, n, -1)
    if fmt == "e4m3":
        vals = words.view(ml_dtypes.float8_e4m3fn).astype(np.float64)
    else:
        nib = np.empty((g, 128, n, 4), np.uint8)
        nib[..., 0::2] = words & 0xF
        nib[..., 1::2] = words >> 4
        vals = E2M1[nib]
    vals = vals * np.repeat(np.exp2(scales.astype(np.float64) - 127.0), 8, axis=1)[..., None]
    return vals.transpose(0, 1, 3, 2).reshape(g * 512, n)


def sigmoid(v):
    return 1.0 / (1.0 + np.exp(-v))


D, T, U, I, J = 512, 1024, 1024, 256, 512


def setup_inputs():
    n = np.random.standard_normal
    idx = np.random.permutation(T)[:I]
    idx2 = np.random.permutation(U)[:J]
    fd = mx_kscale(D)
    tabbp = pack_weight(n((D, U)) / fd[:, None], "e2m1")
    return {
        "taba": (n((D, T)) * 1 / np.sqrt(D) * fd[:, None]).astype(np.float32),
        "dtab": (n((D, T)) * 1.3 / np.sqrt(D) * fd[:, None]).astype(np.float32),
        "tabb_words": tabbp[0],
        "tabb_scales": tabbp[1],
        "steep": (np.random.uniform(0.7, 2.0, (I, 1))).astype(np.float32),
        "bias": (np.random.uniform(-0.7, 0.7, (1, J))).astype(np.float32),
        "degree": (np.random.uniform(0.0, 1.0, (I, J))).astype(np.float32),
        "pw": (np.random.uniform(0.5, 3.0, (1, J))).astype(np.float32),
        "base": (0.3 * n((I, J))).astype(np.float32),
        "offs": striped(idx),
        "offs2": striped(idx2),
    }


def reference(taba, dtab, tabb_words, tabb_scales, steep, bias, degree, pw, base, offs, offs2):
    idx = unstriped(offs)
    idx2 = unstriped(offs2)
    tabbu = unpack_weight(tabb_words, tabb_scales, "e2m1")
    tabaidxq = mxq(f64(taba)[:, idx], 0, "e4m3")
    tabbidx2g = tabbu[:, idx2]
    s = tabaidxq.T @ tabbidx2g
    dtabidxq = mxq(f64(dtab)[:, idx], 0, "e4m3")
    ts = dtabidxq.T @ tabbidx2g
    mg = sigmoid(s * f64(steep) + f64(bias))
    dmg = f64(pw) * (mg - f64(degree)) * 2.0
    xmg = ts * f64(steep) * mg * (1.0 - mg)
    xdmg = xmg * f64(pw) * 2.0
    xds = ((xdmg * mg + xmg * dmg) * (1.0 - mg) + xmg * (-1.0) * dmg * mg) * f64(steep)
    y = xds + f64(base)
    return y

@@ -1,0 +1,170 @@
+from contextlib import ExitStack
+
+import concourse.mybir as mybir
+from concourse.masks import make_identity
+
+D, T, U, I, J = 512, 1024, 1024, 256, 512
+FLOPS = 2 * 2 * D * I * J
+
+F32 = mybir.dt.float32
+BF16 = mybir.dt.bfloat16
+I32 = mybir.dt.int32
+U32 = mybir.dt.uint32
+U16 = mybir.dt.uint16
+U8 = mybir.dt.uint8
+FP8X4 = mybir.dt.float8_e4m3fn_x4
+FP4X4 = mybir.dt.float4_e2m1fn_x4
+ACT = mybir.ActivationFunctionType
+ALU = mybir.AluOpType
+
+P = 128
+PACK = 4
+I_TILES = I // P
+J_BLOCKS = J // P
+HALVES = 2
+J_HALF = J // HALVES
+BLOCKS_PER_HALF = J_BLOCKS // HALVES
+STEEP_AT, BIAS_AT, PW_AT = 0, 4, 8
+
+
+def tile_attend_hvpairfit_kernel(tc, taba, dtab, tabb_words, tabb_scales, steep, bias, degree, pw, base, offs, offs2, out):
+    nc = tc.nc
+    with ExitStack() as ctx:
+        held = ctx.enter_context(tc.tile_pool(name="held", bufs=1))
+        psum = ctx.enter_context(tc.psum_pool(name="psum", bufs=1))
+
+        list_i = held.tile([P, I // 16], U16, name="list_i")
+        list_j = held.tile([P, J // 16], U16, name="list_j")
+        b_words = held.tile([P, U], U16, name="b_words", align_bytes=64)
+        b_scales = held.tile([P, U], U8, name="b_scales", align_bytes=64)
+        a_rows = [held.tile([P, T], F32, name=f"a_rows{t}") for t in range(PACK)]
+        d_rows = [held.tile([P, T], F32, name=f"d_rows{t}") for t in range(PACK)]
+        degree_sb = held.tile([P, I_TILES, J], F32, name="degree_sb")
+        base_sb = held.tile([P, I_TILES, J], F32, name="base_sb")
+        vector_rows = held.tile([P, P], F32, name="vector_rows")
+
+        nc.vector.memset(b_scales[:].bitcast(I32), 0)
+        taba_by_place = taba.rearrange("(p t) n -> p t n", t=PACK)
+        dtab_by_place = dtab.rearrange("(p t) n -> p t n", t=PACK)
+        nc.sync.dma_start(list_j[:], offs2)
+        nc.sync.dma_start(b_words[:].bitcast(I32), tabb_words[0].bitcast(I32))
+        nc.sync.dma_start(list_i[:], offs)
+        for q in range(4):
+            nc.scalar.dma_start(b_scales[32 * q : 32 * q + 4, :].bitcast(I32), tabb_scales[0, 4 * q : 4 * q + 4, :].bitcast(I32))
+        for t in range(PACK):
+            nc.sync.dma_start(a_rows[t][:], taba_by_place[:, t, :])
+        nc.gpsimd.memset(vector_rows[:], 0.0)
+        nc.gpsimd.dma_start(vector_rows[STEEP_AT : STEEP_AT + I_TILES, :], steep.rearrange("(m p) o -> m (p o)", p=P))
+        nc.gpsimd.dma_start(vector_rows[BIAS_AT : BIAS_AT + J_BLOCKS, :], bias.rearrange("o (b p) -> (o b) p", p=P))
+        nc.gpsimd.dma_start(vector_rows[PW_AT : PW_AT + J_BLOCKS, :], pw.rearrange("o (b p) -> (o b) p", p=P))
+        for t in (0, 1):
+            nc.sync.dma_start(d_rows[t][:], dtab_by_place[:, t, :])
+        nc.sync.dma_start(degree_sb[:], degree.rearrange("(m p) j -> p m j", p=P))
+        for t in (2, 3):
+            nc.sync.dma_start(d_rows[t][:], dtab_by_place[:, t, :])
+        nc.sync.dma_start(base_sb[:], base.rearrange("(m p) j -> p m j", p=P))
+
+        identity = held.tile([P, P], F32, name="identity")
+        make_identity(nc, identity[:])
+
+        half_bias = held.tile([P, J_BLOCKS], F32, name="half_bias")
+        half_pw = held.tile([P, J_BLOCKS], F32, name="half_pw")
+        neg_half_pw = held.tile([P, J_BLOCKS], F32, name="neg_half_pw")
+        steep_sq = held.tile([P, I_TILES], F32, name="steep_sq")
+        steep_sb = held.tile([P, I_TILES], F32, name="steep_sb")
+        columns = psum.tile([P, P], F32, name="columns", tag="tangent0")
+        nc.tensor.transpose(columns[:], vector_rows[:], identity[:])
+        nc.scalar.copy(steep_sb[:], columns[:, STEEP_AT : STEEP_AT + I_TILES])
+        nc.scalar.activation(half_bias[:], columns[:, BIAS_AT : BIAS_AT + J_BLOCKS], ACT.Copy, scale=0.5)
+        nc.scalar.activation(steep_sq[:], columns[:, STEEP_AT : STEEP_AT + I_TILES], ACT.Square)
+        nc.scalar.activation(half_pw[:], columns[:, PW_AT : PW_AT + J_BLOCKS], ACT.Copy, scale=0.5)
+        nc.scalar.activation(neg_half_pw[:], columns[:, PW_AT : PW_AT + J_BLOCKS], ACT.Copy, scale=-0.5)
+
+        bj_words = held.tile([P, J], U16, name="bj_words", align_bytes=64)
+        bj_scales = held.tile([P, J], U8, name="bj_scales", align_bytes=64)
+        nc.vector.tensor_copy(bj_words[:], b_words[:].indirect(list_j[:]))
+        nc.vector.tensor_copy(bj_scales[:], b_scales[:].indirect(list_j[:]))
+
+        def gather_plane(woven, rows, t):
+            nc.vector.tensor_copy(woven[:, :, t], rows[t][:].indirect(list_i[:]))
+
+        def quantise(woven, name):
+            codes = held.tile([P, I], U32, name=name + "_codes", align_bytes=64)
+            scales = held.tile([P, I], U8, name=name + "_scales", align_bytes=64)
+            nc.vector.quantize_mx(out=codes[:].bitcast(FP8X4), scales=scales[:], in_=woven[:].rearrange("p n t -> p (n t)"))
+            return codes, scales
+
+        a_woven = held.tile([P, I, PACK], BF16, name="a_woven", align_bytes=64)
+        d_woven = held.tile([P, I, PACK], BF16, name="d_woven", align_bytes=64)
+        for t in range(PACK):
+            gather_plane(a_woven, a_rows, t)
+        a_codes, a_scales = quantise(a_woven, "a")
+
+        score = [psum.tile([P, I_TILES, J_HALF], F32, name=f"score{h}", tag=f"ij{h}") for h in range(HALVES)]
+        scaled = [held.tile([P, I_TILES, J_HALF], F32, name=f"scaled{h}") for h in range(HALVES)]
+        logit = [psum.tile([P, BLOCKS_PER_HALF, I], F32, name=f"logit{h}") for h in range(HALVES)]
+        degree_t = [psum.tile([P, BLOCKS_PER_HALF, I], F32, name=f"degree_t{h}") for h in range(HALVES)]
+        for h in range(HALVES):
+            js = slice(h * J_HALF, (h + 1) * J_HALF)
+            for m in range(I_TILES):
+                ms = slice(m * P, (m + 1) * P)
+                nc.tensor.matmul_mx(out=score[h][:, m, :], lhsT=a_codes[:, ms].bitcast(FP8X4), lhsT_scale=a_scales[:, ms],
+                                    rhs=bj_words[:, js].bitcast(FP4X4), rhs_scale=bj_scales[:, js], start=True, stop=True)
+        tanh = [held.tile([P, BLOCKS_PER_HALF, I], F32, name=f"tanh{h}") for h in range(HALVES)]
+        for h in range(HALVES):
+            for m in range(I_TILES):
+                nc.scalar.activation(scaled[h][:, m, :], score[h][:, m, :], ACT.Copy, scale=steep_sb[:, m : m + 1])
+            for b in range(BLOCKS_PER_HALF):
+                for m in range(I_TILES):
+                    nc.tensor.transpose(logit[h][:, b, m * P : (m + 1) * P], scaled[h][:, m, b * P : (b + 1) * P], identity[:])
+        for t in (0, 1):
+            gather_plane(d_woven, d_rows, t)
+        for h in range(HALVES):
+            for b in range(BLOCKS_PER_HALF):
+                j0 = h * J_HALF + b * P
+                for m in range(I_TILES):
+                    nc.tensor.transpose(degree_t[h][:, b, m * P : (m + 1) * P], degree_sb[:, m, j0 : j0 + P], identity[:])
+
+        slope = [held.tile([P, BLOCKS_PER_HALF, I], F32, name=f"slope{h}") for h in range(HALVES)]
+        poly = [held.tile([P, BLOCKS_PER_HALF, I], F32, name=f"poly{h}") for h in range(HALVES)]
+        for h in range(HALVES):
+            for b in range(BLOCKS_PER_HALF):
+                col = h * BLOCKS_PER_HALF + b
+                nc.scalar.activation(tanh[h][:, b, :], logit[h][:, b, :], ACT.Tanh, bias=half_bias[:, col : col + 1], scale=0.5)
+        for h in range(HALVES):
+            tanh_sq = held.tile([P, BLOCKS_PER_HALF, I], F32, name=f"tanh_sq{h}")
+            nc.scalar.activation(tanh_sq[:], tanh[h][:], ACT.Square)
+            for b in range(BLOCKS_PER_HALF):
+                col = h * BLOCKS_PER_HALF + b
+                nc.scalar.activation(slope[h][:, b, :], tanh_sq[:, b, :], ACT.Identity,
+                                     bias=neg_half_pw[:, col : col + 1], scale=half_pw[:, col : col + 1])
+        inner = [held.tile([P, BLOCKS_PER_HALF, I], F32, name=f"inner{h}") for h in range(HALVES)]
+        for h in range(HALVES):
+            nc.vector.scalar_tensor_tensor(inner[h][:], tanh[h][:], 0.75, degree_t[h][:], ALU.mult, ALU.subtract)
+            nc.vector.scalar_tensor_tensor(poly[h][:], inner[h][:], 0.5, tanh[h][:], ALU.add, ALU.mult)
+            gather_plane(d_woven, d_rows, 2 + h)
+        d_codes, d_scales = quantise(d_woven, "d")
+
+        tangent = [psum.tile([P, BLOCKS_PER_HALF, I], F32, name=f"tangent{h}", tag=f"tangent{h}") for h in range(HALVES)]
+        for h in range(HALVES):
+            for b in range(BLOCKS_PER_HALF):
+                js = slice(h * J_HALF + b * P, h * J_HALF + (b + 1) * P)
+                nc.tensor.matmul_mx(out=tangent[h][:, b, :], lhsT=bj_words[:, js].bitcast(FP4X4), lhsT_scale=bj_scales[:, js],
+                                    rhs=d_codes[:].bitcast(FP8X4), rhs_scale=d_scales[:], start=True, stop=True)
+        factor = [held.tile([P, BLOCKS_PER_HALF, I], F32, name=f"factor{h}") for h in range(HALVES)]
+        change = [held.tile([P, BLOCKS_PER_HALF, I], F32, name=f"change{h}") for h in range(HALVES)]
+        for h in range(HALVES):
+            nc.vector.scalar_tensor_tensor(factor[h][:], poly[h][:], -0.25, slope[h][:], ALU.add, ALU.mult)
+        for h in range(HALVES):
+            nc.vector.tensor_tensor(change[h][:], tangent[h][:], factor[h][:], ALU.mult)
+        out_by_tile = out.rearrange("(m p) j -> p m j", p=P)
+        for h in range(HALVES):
+            js = slice(h * J_HALF, (h + 1) * J_HALF)
+            turned = psum.tile([P, I_TILES, J_HALF], F32, name=f"turned{h}", tag=f"ij{h}")
+            for m in range(I_TILES):
+                for b in range(BLOCKS_PER_HALF):
+                    nc.tensor.transpose(turned[:, m, b * P : (b + 1) * P], change[h][:, b, m * P : (m + 1) * P], identity[:])
+            for m in range(I_TILES):
+                result = held.tile([P, J_HALF], F32, name=f"result{h}{m}")
+                nc.vector.scalar_tensor_tensor(result[:], turned[:, m, :], steep_sq[:, m : m + 1], base_sb[:, m, js], ALU.mult, ALU.add)
+                nc.sync.dma_start(out_by_tile[:, m, js], result[:])

@@ -24,7 +24,8 @@ J_BLOCKS = J // P
 HALVES = 2
 J_HALF = J // HALVES
 BLOCKS_PER_HALF = J_BLOCKS // HALVES
-STEEP_AT, BIAS_AT, PW_AT = 0, 4, 8
+A_FIRST = 1280
+BIAS_AT, PW_AT = 0, 4
 
 
 def tile_attend_hvpairfit_kernel(tc, taba, dtab, tabb_words, tabb_scales, steep, bias, degree, pw, base, offs, offs2, out):
@@ -37,48 +38,44 @@ def tile_attend_hvpairfit_kernel(tc, taba, dtab, tabb_words, tabb_scales, steep,
         list_j = held.tile([P, J // 16], U16, name="list_j")
         b_words = held.tile([P, U], U16, name="b_words", align_bytes=64)
         b_scales = held.tile([P, U], U8, name="b_scales", align_bytes=64)
-        a_rows = [held.tile([P, T], F32, name=f"a_rows{t}") for t in range(PACK)]
-        d_rows = [held.tile([P, T], F32, name=f"d_rows{t}") for t in range(PACK)]
-        degree_sb = held.tile([P, I_TILES, J], F32, name="degree_sb")
+        a_table = held.tile([P, PACK * T], F32, name="a_table")
+        d_loads = [held.tile([P, T], F32, name=f"d_rows{t}") for t in range(PACK)]
+        a_rows = [a_table[:, t * T : (t + 1) * T] for t in range(PACK)]
+        d_rows = [tile[:] for tile in d_loads]
+        degree_sb = [held.tile([P, I_TILES, J_HALF], F32, name=f"degree_sb{h}") for h in range(HALVES)]
         base_sb = held.tile([P, I_TILES, J], F32, name="base_sb")
         vector_rows = held.tile([P, P], F32, name="vector_rows")
 
-        nc.vector.memset(b_scales[:].bitcast(I32), 0)
-        taba_by_place = taba.rearrange("(p t) n -> p t n", t=PACK)
-        dtab_by_place = dtab.rearrange("(p t) n -> p t n", t=PACK)
-        nc.sync.dma_start(list_j[:], offs2)
-        nc.sync.dma_start(b_words[:].bitcast(I32), tabb_words[0].bitcast(I32))
-        nc.sync.dma_start(list_i[:], offs)
-        for q in range(4):
-            nc.scalar.dma_start(b_scales[32 * q : 32 * q + 4, :].bitcast(I32), tabb_scales[0, 4 * q : 4 * q + 4, :].bitcast(I32))
-        for t in range(PACK):
-            nc.sync.dma_start(a_rows[t][:], taba_by_place[:, t, :])
+        nc.gpsimd.memset(b_scales[:].bitcast(I32), 0)
         nc.gpsimd.memset(vector_rows[:], 0.0)
-        nc.gpsimd.dma_start(vector_rows[STEEP_AT : STEEP_AT + I_TILES, :], steep.rearrange("(m p) o -> m (p o)", p=P))
-        nc.gpsimd.dma_start(vector_rows[BIAS_AT : BIAS_AT + J_BLOCKS, :], bias.rearrange("o (b p) -> (o b) p", p=P))
-        nc.gpsimd.dma_start(vector_rows[PW_AT : PW_AT + J_BLOCKS, :], pw.rearrange("o (b p) -> (o b) p", p=P))
-        for t in (0, 1):
-            nc.sync.dma_start(d_rows[t][:], dtab_by_place[:, t, :])
-        nc.sync.dma_start(degree_sb[:], degree.rearrange("(m p) j -> p m j", p=P))
-        for t in (2, 3):
-            nc.sync.dma_start(d_rows[t][:], dtab_by_place[:, t, :])
-        nc.sync.dma_start(base_sb[:], base.rearrange("(m p) j -> p m j", p=P))
-
         identity = held.tile([P, P], F32, name="identity")
         make_identity(nc, identity[:])
-
-        half_bias = held.tile([P, J_BLOCKS], F32, name="half_bias")
-        half_pw = held.tile([P, J_BLOCKS], F32, name="half_pw")
-        neg_half_pw = held.tile([P, J_BLOCKS], F32, name="neg_half_pw")
-        steep_sq = held.tile([P, I_TILES], F32, name="steep_sq")
         steep_sb = held.tile([P, I_TILES], F32, name="steep_sb")
-        columns = psum.tile([P, P], F32, name="columns", tag="tangent0")
-        nc.tensor.transpose(columns[:], vector_rows[:], identity[:])
-        nc.scalar.copy(steep_sb[:], columns[:, STEEP_AT : STEEP_AT + I_TILES])
-        nc.scalar.activation(half_bias[:], columns[:, BIAS_AT : BIAS_AT + J_BLOCKS], ACT.Copy, scale=0.5)
-        nc.scalar.activation(steep_sq[:], columns[:, STEEP_AT : STEEP_AT + I_TILES], ACT.Square)
-        nc.scalar.activation(half_pw[:], columns[:, PW_AT : PW_AT + J_BLOCKS], ACT.Copy, scale=0.5)
-        nc.scalar.activation(neg_half_pw[:], columns[:, PW_AT : PW_AT + J_BLOCKS], ACT.Copy, scale=-0.5)
+        with nc.allow_non_contiguous_dma(reason="one value a partition"):
+            nc.gpsimd.dma_start(steep_sb[:], steep.rearrange("(m p) o -> p (m o)", p=P))
+
+        taba_by_place = taba.rearrange("(p t) n -> p (t n)", t=PACK)
+        dtab_by_place = dtab.rearrange("(p t) n -> p t n", t=PACK)
+        degree_by_tile = degree.rearrange("(m p) j -> p m j", p=P)
+        nc.sync.dma_start(list_j[:], offs2)
+        nc.sync.dma_start(b_words[:].bitcast(I32), tabb_words[0].bitcast(I32))
+        nc.sync.dma_start(a_table[:, 0:A_FIRST], taba_by_place[:, 0:A_FIRST])
+        for q in range(4):
+            nc.sync.dma_start(b_scales[32 * q : 32 * q + 4, :].bitcast(I32), tabb_scales[0, 4 * q : 4 * q + 4, :].bitcast(I32))
+        nc.sync.dma_start(list_i[:], offs)
+        for c0, c1 in ((A_FIRST, 2 * T), (2 * T, 3 * T), (3 * T, 4 * T)):
+            nc.sync.dma_start(a_table[:, c0:c1], taba_by_place[:, c0:c1])
+        nc.sync.dma_start(d_rows[0], dtab_by_place[:, 0, :])
+        nc.sync.dma_start(vector_rows[BIAS_AT : BIAS_AT + J_BLOCKS, :], bias.rearrange("o (b p) -> (o b) p", p=P))
+        nc.sync.dma_start(vector_rows[PW_AT : PW_AT + J_BLOCKS, :], pw.rearrange("o (b p) -> (o b) p", p=P))
+        nc.sync.dma_start(d_rows[1], dtab_by_place[:, 1, :])
+        for h in range(HALVES):
+            nc.sync.dma_start(d_rows[2 + h], dtab_by_place[:, 2 + h, :])
+            nc.sync.dma_start(degree_sb[h][:], degree_by_tile[:, :, h * J_HALF : (h + 1) * J_HALF])
+        nc.sync.dma_start(base_sb[:], base.rearrange("(m p) j -> p m j", p=P))
+
+        steep_sq = held.tile([P, I_TILES], F32, name="steep_sq")
+        nc.scalar.activation(steep_sq[:], steep_sb[:], ACT.Square)
 
         bj_words = held.tile([P, J], U16, name="bj_words", align_bytes=64)
         bj_scales = held.tile([P, J], U8, name="bj_scales", align_bytes=64)
@@ -86,7 +83,7 @@ def tile_attend_hvpairfit_kernel(tc, taba, dtab, tabb_words, tabb_scales, steep,
         nc.vector.tensor_copy(bj_scales[:], b_scales[:].indirect(list_j[:]))
 
         def gather_plane(woven, rows, t):
-            nc.vector.tensor_copy(woven[:, :, t], rows[t][:].indirect(list_i[:]))
+            nc.vector.tensor_copy(woven[:, :, t], rows[t].indirect(list_i[:]))
 
         def quantise(woven, name):
             codes = held.tile([P, I], U32, name=name + "_codes", align_bytes=64)
@@ -96,34 +93,45 @@ def tile_attend_hvpairfit_kernel(tc, taba, dtab, tabb_words, tabb_scales, steep,
 
         a_woven = held.tile([P, I, PACK], BF16, name="a_woven", align_bytes=64)
         d_woven = held.tile([P, I, PACK], BF16, name="d_woven", align_bytes=64)
-        for t in range(PACK):
+        a_pair = held.tile([P, 2, I], F32, name="a_pair")
+        for t in (0, 1):
+            nc.vector.tensor_copy(a_pair[:, t, :], a_rows[t].indirect(list_i[:]))
+        nc.scalar.copy(a_woven[:, :, 0:2], a_pair[:].rearrange("p t n -> p n t"))
+        for t in (2, 3):
             gather_plane(a_woven, a_rows, t)
         a_codes, a_scales = quantise(a_woven, "a")
 
-        score = [psum.tile([P, I_TILES, J_HALF], F32, name=f"score{h}", tag=f"ij{h}") for h in range(HALVES)]
+        score = [[psum.tile([P, J_HALF], F32, name=f"score{h}{m}", tag=f"early{h}{m}") for m in range(I_TILES)] for h in range(HALVES)]
         scaled = [held.tile([P, I_TILES, J_HALF], F32, name=f"scaled{h}") for h in range(HALVES)]
         logit = [psum.tile([P, BLOCKS_PER_HALF, I], F32, name=f"logit{h}") for h in range(HALVES)]
-        degree_t = [psum.tile([P, BLOCKS_PER_HALF, I], F32, name=f"degree_t{h}") for h in range(HALVES)]
         for h in range(HALVES):
             js = slice(h * J_HALF, (h + 1) * J_HALF)
             for m in range(I_TILES):
                 ms = slice(m * P, (m + 1) * P)
-                nc.tensor.matmul_mx(out=score[h][:, m, :], lhsT=a_codes[:, ms].bitcast(FP8X4), lhsT_scale=a_scales[:, ms],
+                nc.tensor.matmul_mx(out=score[h][m][:], lhsT=a_codes[:, ms].bitcast(FP8X4), lhsT_scale=a_scales[:, ms],
                                     rhs=bj_words[:, js].bitcast(FP4X4), rhs_scale=bj_scales[:, js], start=True, stop=True)
+        half_bias = held.tile([P, J_BLOCKS], F32, name="half_bias")
+        half_pw = held.tile([P, J_BLOCKS], F32, name="half_pw")
+        neg_half_pw = held.tile([P, J_BLOCKS], F32, name="neg_half_pw")
+        columns = psum.tile([P, P], F32, name="columns", tag="tangent0")
+        nc.tensor.transpose(columns[:], vector_rows[:], identity[:])
         tanh = [held.tile([P, BLOCKS_PER_HALF, I], F32, name=f"tanh{h}") for h in range(HALVES)]
         for h in range(HALVES):
             for m in range(I_TILES):
-                nc.scalar.activation(scaled[h][:, m, :], score[h][:, m, :], ACT.Copy, scale=steep_sb[:, m : m + 1])
+                nc.scalar.activation(scaled[h][:, m, :], score[h][m][:], ACT.Copy, scale=steep_sb[:, m : m + 1])
             for b in range(BLOCKS_PER_HALF):
                 for m in range(I_TILES):
                     nc.tensor.transpose(logit[h][:, b, m * P : (m + 1) * P], scaled[h][:, m, b * P : (b + 1) * P], identity[:])
-        for t in (0, 1):
+        nc.scalar.activation(half_bias[:], columns[:, BIAS_AT : BIAS_AT + J_BLOCKS], ACT.Copy, scale=0.5)
+        nc.scalar.activation(half_pw[:], columns[:, PW_AT : PW_AT + J_BLOCKS], ACT.Copy, scale=0.5)
+        nc.scalar.activation(neg_half_pw[:], columns[:, PW_AT : PW_AT + J_BLOCKS], ACT.Copy, scale=-0.5)
+        for t in (0, 1, 2):
             gather_plane(d_woven, d_rows, t)
+        degree_t = [psum.tile([P, BLOCKS_PER_HALF, I], F32, name=f"degree_t{h}", tag=f"early0{h}") for h in range(HALVES)]
         for h in range(HALVES):
             for b in range(BLOCKS_PER_HALF):
-                j0 = h * J_HALF + b * P
                 for m in range(I_TILES):
-                    nc.tensor.transpose(degree_t[h][:, b, m * P : (m + 1) * P], degree_sb[:, m, j0 : j0 + P], identity[:])
+                    nc.tensor.transpose(degree_t[h][:, b, m * P : (m + 1) * P], degree_sb[h][:, m, b * P : (b + 1) * P], identity[:])
 
         slope = [held.tile([P, BLOCKS_PER_HALF, I], F32, name=f"slope{h}") for h in range(HALVES)]
         poly = [held.tile([P, BLOCKS_PER_HALF, I], F32, name=f"poly{h}") for h in range(HALVES)]
@@ -138,12 +146,13 @@ def tile_attend_hvpairfit_kernel(tc, taba, dtab, tabb_words, tabb_scales, steep,
                 col = h * BLOCKS_PER_HALF + b
                 nc.scalar.activation(slope[h][:, b, :], tanh_sq[:, b, :], ACT.Identity,
                                      bias=neg_half_pw[:, col : col + 1], scale=half_pw[:, col : col + 1])
-        inner = [held.tile([P, BLOCKS_PER_HALF, I], F32, name=f"inner{h}") for h in range(HALVES)]
         for h in range(HALVES):
-            nc.vector.scalar_tensor_tensor(inner[h][:], tanh[h][:], 0.75, degree_t[h][:], ALU.mult, ALU.subtract)
-            nc.vector.scalar_tensor_tensor(poly[h][:], inner[h][:], 0.5, tanh[h][:], ALU.add, ALU.mult)
-            gather_plane(d_woven, d_rows, 2 + h)
-        d_codes, d_scales = quantise(d_woven, "d")
+            inner = held.tile([P, BLOCKS_PER_HALF, I], F32, name=f"inner{h}")
+            nc.vector.scalar_tensor_tensor(inner[:], tanh[h][:], 0.75, degree_t[h][:], ALU.mult, ALU.subtract)
+            nc.vector.scalar_tensor_tensor(poly[h][:], inner[:], 0.5, tanh[h][:], ALU.add, ALU.mult)
+            if h == 0:
+                gather_plane(d_woven, d_rows, 3)
+                d_codes, d_scales = quantise(d_woven, "d")
 
         tangent = [psum.tile([P, BLOCKS_PER_HALF, I], F32, name=f"tangent{h}", tag=f"tangent{h}") for h in range(HALVES)]
         for h in range(HALVES):
@@ -151,7 +160,7 @@ def tile_attend_hvpairfit_kernel(tc, taba, dtab, tabb_words, tabb_scales, steep,
                 js = slice(h * J_HALF + b * P, h * J_HALF + (b + 1) * P)
                 nc.tensor.matmul_mx(out=tangent[h][:, b, :], lhsT=bj_words[:, js].bitcast(FP4X4), lhsT_scale=bj_scales[:, js],
                                     rhs=d_codes[:].bitcast(FP8X4), rhs_scale=d_scales[:], start=True, stop=True)
-        factor = [held.tile([P, BLOCKS_PER_HALF, I], F32, name=f"factor{h}") for h in range(HALVES)]
+        factor = [held.tile([P, BLOCKS_PER_HALF, I], F32, name=f"factor{h}", tag=f"factor{h}") for h in range(HALVES)]
         change = [held.tile([P, BLOCKS_PER_HALF, I], F32, name=f"change{h}") for h in range(HALVES)]
         for h in range(HALVES):
             nc.vector.scalar_tensor_tensor(factor[h][:], poly[h][:], -0.25, slope[h][:], ALU.add, ALU.mult)
@@ -160,11 +169,11 @@ def tile_attend_hvpairfit_kernel(tc, taba, dtab, tabb_words, tabb_scales, steep,
         out_by_tile = out.rearrange("(m p) j -> p m j", p=P)
         for h in range(HALVES):
             js = slice(h * J_HALF, (h + 1) * J_HALF)
-            turned = psum.tile([P, I_TILES, J_HALF], F32, name=f"turned{h}", tag=f"ij{h}")
+            turned = psum.tile([P, I_TILES, J_HALF], F32, name=f"turned{h}", tag=f"early1{h}")
             for m in range(I_TILES):
                 for b in range(BLOCKS_PER_HALF):
                     nc.tensor.transpose(turned[:, m, b * P : (b + 1) * P], change[h][:, b, m * P : (m + 1) * P], identity[:])
             for m in range(I_TILES):
-                result = held.tile([P, J_HALF], F32, name=f"result{h}{m}")
+                result = held.tile([P, J_HALF], F32, name=f"result{h}{m}", tag=f"factor{HALVES - 1}" if h + m == 0 else f"result{h}{m}")
                 nc.vector.scalar_tensor_tensor(result[:], turned[:, m, :], steep_sq[:, m : m + 1], base_sb[:, m, js], ALU.mult, ALU.add)
                 nc.sync.dma_start(out_by_tile[:, m, js], result[:])

@@ -26,6 +26,7 @@ J_HALF = J // HALVES
 BLOCKS_PER_HALF = J_BLOCKS // HALVES
 A_FIRST = 1280
 BIAS_AT, PW_AT = 0, 4
+TURNED_BANKS = (("early11", "logit0"), ("logit1", "early00"))
 
 
 def tile_attend_hvpairfit_kernel(tc, taba, dtab, tabb_words, tabb_scales, steep, bias, degree, pw, base, offs, offs2, out):
@@ -68,9 +69,9 @@ def tile_attend_hvpairfit_kernel(tc, taba, dtab, tabb_words, tabb_scales, steep,
         nc.sync.dma_start(d_rows[0], dtab_by_place[:, 0, :])
         nc.sync.dma_start(vector_rows[BIAS_AT : BIAS_AT + J_BLOCKS, :], bias.rearrange("o (b p) -> (o b) p", p=P))
         nc.sync.dma_start(vector_rows[PW_AT : PW_AT + J_BLOCKS, :], pw.rearrange("o (b p) -> (o b) p", p=P))
-        nc.sync.dma_start(d_rows[1], dtab_by_place[:, 1, :])
+        for t in (1, 2, 3):
+            nc.sync.dma_start(d_rows[t], dtab_by_place[:, t, :])
         for h in range(HALVES):
-            nc.sync.dma_start(d_rows[2 + h], dtab_by_place[:, 2 + h, :])
             nc.sync.dma_start(degree_sb[h][:], degree_by_tile[:, :, h * J_HALF : (h + 1) * J_HALF])
         nc.sync.dma_start(base_sb[:], base.rearrange("(m p) j -> p m j", p=P))
 
@@ -103,7 +104,7 @@ def tile_attend_hvpairfit_kernel(tc, taba, dtab, tabb_words, tabb_scales, steep,
 
         score = [[psum.tile([P, J_HALF], F32, name=f"score{h}{m}", tag=f"early{h}{m}") for m in range(I_TILES)] for h in range(HALVES)]
         scaled = [held.tile([P, I_TILES, J_HALF], F32, name=f"scaled{h}") for h in range(HALVES)]
-        logit = [psum.tile([P, BLOCKS_PER_HALF, I], F32, name=f"logit{h}") for h in range(HALVES)]
+        logit = [psum.tile([P, BLOCKS_PER_HALF, I], F32, name=f"logit{h}", tag=f"logit{h}") for h in range(HALVES)]
         for h in range(HALVES):
             js = slice(h * J_HALF, (h + 1) * J_HALF)
             for m in range(I_TILES):
@@ -125,13 +126,16 @@ def tile_attend_hvpairfit_kernel(tc, taba, dtab, tabb_words, tabb_scales, steep,
         nc.scalar.activation(half_bias[:], columns[:, BIAS_AT : BIAS_AT + J_BLOCKS], ACT.Copy, scale=0.5)
         nc.scalar.activation(half_pw[:], columns[:, PW_AT : PW_AT + J_BLOCKS], ACT.Copy, scale=0.5)
         nc.scalar.activation(neg_half_pw[:], columns[:, PW_AT : PW_AT + J_BLOCKS], ACT.Copy, scale=-0.5)
-        for t in (0, 1, 2):
+        for t in range(PACK):
             gather_plane(d_woven, d_rows, t)
-        degree_t = [psum.tile([P, BLOCKS_PER_HALF, I], F32, name=f"degree_t{h}", tag=f"early0{h}") for h in range(HALVES)]
+        d_codes, d_scales = quantise(d_woven, "d")
+        degree_first = [psum.tile([P, I], F32, name=f"degree_first{b}", tag=f"early0{b}") for b in range(BLOCKS_PER_HALF)]
+        degree_second = psum.tile([P, BLOCKS_PER_HALF, I], F32, name="degree_second", tag="early10")
         for h in range(HALVES):
             for b in range(BLOCKS_PER_HALF):
+                target = degree_first[b][:] if h == 0 else degree_second[:, b, :]
                 for m in range(I_TILES):
-                    nc.tensor.transpose(degree_t[h][:, b, m * P : (m + 1) * P], degree_sb[h][:, m, b * P : (b + 1) * P], identity[:])
+                    nc.tensor.transpose(target[:, m * P : (m + 1) * P], degree_sb[h][:, m, b * P : (b + 1) * P], identity[:])
 
         slope = [held.tile([P, BLOCKS_PER_HALF, I], F32, name=f"slope{h}") for h in range(HALVES)]
         poly = [held.tile([P, BLOCKS_PER_HALF, I], F32, name=f"poly{h}") for h in range(HALVES)]
@@ -146,13 +150,12 @@ def tile_attend_hvpairfit_kernel(tc, taba, dtab, tabb_words, tabb_scales, steep,
                 col = h * BLOCKS_PER_HALF + b
                 nc.scalar.activation(slope[h][:, b, :], tanh_sq[:, b, :], ACT.Identity,
                                      bias=neg_half_pw[:, col : col + 1], scale=half_pw[:, col : col + 1])
+        inner = [held.tile([P, BLOCKS_PER_HALF, I], F32, name=f"inner{h}") for h in range(HALVES)]
+        for b in range(BLOCKS_PER_HALF):
+            nc.vector.scalar_tensor_tensor(inner[0][:, b, :], tanh[0][:, b, :], 0.75, degree_first[b][:], ALU.mult, ALU.subtract)
+        nc.vector.scalar_tensor_tensor(inner[1][:], tanh[1][:], 0.75, degree_second[:], ALU.mult, ALU.subtract)
         for h in range(HALVES):
-            inner = held.tile([P, BLOCKS_PER_HALF, I], F32, name=f"inner{h}")
-            nc.vector.scalar_tensor_tensor(inner[:], tanh[h][:], 0.75, degree_t[h][:], ALU.mult, ALU.subtract)
-            nc.vector.scalar_tensor_tensor(poly[h][:], inner[:], 0.5, tanh[h][:], ALU.add, ALU.mult)
-            if h == 0:
-                gather_plane(d_woven, d_rows, 3)
-                d_codes, d_scales = quantise(d_woven, "d")
+            nc.vector.scalar_tensor_tensor(poly[h][:], inner[h][:], 0.5, tanh[h][:], ALU.add, ALU.mult)
 
         tangent = [psum.tile([P, BLOCKS_PER_HALF, I], F32, name=f"tangent{h}", tag=f"tangent{h}") for h in range(HALVES)]
         for h in range(HALVES):
@@ -169,11 +172,11 @@ def tile_attend_hvpairfit_kernel(tc, taba, dtab, tabb_words, tabb_scales, steep,
         out_by_tile = out.rearrange("(m p) j -> p m j", p=P)
         for h in range(HALVES):
             js = slice(h * J_HALF, (h + 1) * J_HALF)
-            turned = psum.tile([P, I_TILES, J_HALF], F32, name=f"turned{h}", tag=f"early1{h}")
+            turned = [psum.tile([P, J_HALF], F32, name=f"turned{h}{m}", tag=TURNED_BANKS[h][m]) for m in range(I_TILES)]
             for m in range(I_TILES):
                 for b in range(BLOCKS_PER_HALF):
-                    nc.tensor.transpose(turned[:, m, b * P : (b + 1) * P], change[h][:, b, m * P : (m + 1) * P], identity[:])
+                    nc.tensor.transpose(turned[m][:, b * P : (b + 1) * P], change[h][:, b, m * P : (m + 1) * P], identity[:])
             for m in range(I_TILES):
                 result = held.tile([P, J_HALF], F32, name=f"result{h}{m}", tag=f"factor{HALVES - 1}" if h + m == 0 else f"result{h}{m}")
-                nc.vector.scalar_tensor_tensor(result[:], turned[:, m, :], steep_sq[:, m : m + 1], base_sb[:, m, js], ALU.mult, ALU.add)
+                nc.vector.scalar_tensor_tensor(result[:], turned[m][:], steep_sq[:, m : m + 1], base_sb[:, m, js], ALU.mult, ALU.add)
                 nc.sync.dma_start(out_by_tile[:, m, js], result[:])

@@ -47,7 +47,7 @@ def tile_attend_hvpairfit_kernel(tc, taba, dtab, tabb_words, tabb_scales, steep,
         base_sb = held.tile([P, I_TILES, J], F32, name="base_sb")
         vector_rows = held.tile([P, P], F32, name="vector_rows")
 
-        nc.gpsimd.memset(b_scales[:].bitcast(I32), 0)
+        nc.vector.memset(b_scales[:].bitcast(I32), 0)
         nc.gpsimd.memset(vector_rows[:], 0.0)
         identity = held.tile([P, P], F32, name="identity")
         make_identity(nc, identity[:])

from contextlib import ExitStack

import concourse.mybir as mybir
from concourse.masks import make_identity

D, T, U, I, J = 512, 1024, 1024, 256, 512
FLOPS = 2 * 2 * D * I * J

F32 = mybir.dt.float32
BF16 = mybir.dt.bfloat16
I32 = mybir.dt.int32
U32 = mybir.dt.uint32
U16 = mybir.dt.uint16
U8 = mybir.dt.uint8
FP8X4 = mybir.dt.float8_e4m3fn_x4
FP4X4 = mybir.dt.float4_e2m1fn_x4
ACT = mybir.ActivationFunctionType
ALU = mybir.AluOpType

P = 128
PACK = 4
I_TILES = I // P
J_BLOCKS = J // P
HALVES = 2
J_HALF = J // HALVES
BLOCKS_PER_HALF = J_BLOCKS // HALVES
A_FIRST = 1280
BIAS_AT, PW_AT = 0, 4
TURNED_BANKS = (("early11", "logit0"), ("logit1", "early00"))


def tile_attend_hvpairfit_kernel(tc, taba, dtab, tabb_words, tabb_scales, steep, bias, degree, pw, base, offs, offs2, out):
    nc = tc.nc
    with ExitStack() as ctx:
        held = ctx.enter_context(tc.tile_pool(name="held", bufs=1))
        psum = ctx.enter_context(tc.psum_pool(name="psum", bufs=1))

        list_i = held.tile([P, I // 16], U16, name="list_i")
        list_j = held.tile([P, J // 16], U16, name="list_j")
        b_words = held.tile([P, U], U16, name="b_words", align_bytes=64)
        b_scales = held.tile([P, U], U8, name="b_scales", align_bytes=64)
        a_table = held.tile([P, PACK * T], F32, name="a_table")
        d_loads = [held.tile([P, T], F32, name=f"d_rows{t}") for t in range(PACK)]
        a_rows = [a_table[:, t * T : (t + 1) * T] for t in range(PACK)]
        d_rows = [tile[:] for tile in d_loads]
        degree_sb = [held.tile([P, I_TILES, J_HALF], F32, name=f"degree_sb{h}") for h in range(HALVES)]
        base_sb = held.tile([P, I_TILES, J], F32, name="base_sb")
        vector_rows = held.tile([P, P], F32, name="vector_rows")

        nc.vector.memset(b_scales[:].bitcast(I32), 0)
        nc.gpsimd.memset(vector_rows[:], 0.0)
        identity = held.tile([P, P], F32, name="identity")
        make_identity(nc, identity[:])
        steep_sb = held.tile([P, I_TILES], F32, name="steep_sb")
        with nc.allow_non_contiguous_dma(reason="one value a partition"):
            nc.gpsimd.dma_start(steep_sb[:], steep.rearrange("(m p) o -> p (m o)", p=P))

        taba_by_place = taba.rearrange("(p t) n -> p (t n)", t=PACK)
        dtab_by_place = dtab.rearrange("(p t) n -> p t n", t=PACK)
        degree_by_tile = degree.rearrange("(m p) j -> p m j", p=P)
        nc.sync.dma_start(list_j[:], offs2)
        nc.sync.dma_start(b_words[:].bitcast(I32), tabb_words[0].bitcast(I32))
        nc.sync.dma_start(a_table[:, 0:A_FIRST], taba_by_place[:, 0:A_FIRST])
        for q in range(4):
            nc.sync.dma_start(b_scales[32 * q : 32 * q + 4, :].bitcast(I32), tabb_scales[0, 4 * q : 4 * q + 4, :].bitcast(I32))
        nc.sync.dma_start(list_i[:], offs)
        for c0, c1 in ((A_FIRST, 2 * T), (2 * T, 3 * T), (3 * T, 4 * T)):
            nc.sync.dma_start(a_table[:, c0:c1], taba_by_place[:, c0:c1])
        nc.sync.dma_start(d_rows[0], dtab_by_place[:, 0, :])
        nc.sync.dma_start(vector_rows[BIAS_AT : BIAS_AT + J_BLOCKS, :], bias.rearrange("o (b p) -> (o b) p", p=P))
        nc.sync.dma_start(vector_rows[PW_AT : PW_AT + J_BLOCKS, :], pw.rearrange("o (b p) -> (o b) p", p=P))
        for t in (1, 2, 3):
            nc.sync.dma_start(d_rows[t], dtab_by_place[:, t, :])
        for h in range(HALVES):
            nc.sync.dma_start(degree_sb[h][:], degree_by_tile[:, :, h * J_HALF : (h + 1) * J_HALF])
        nc.sync.dma_start(base_sb[:], base.rearrange("(m p) j -> p m j", p=P))

        steep_sq = held.tile([P, I_TILES], F32, name="steep_sq")
        nc.scalar.activation(steep_sq[:], steep_sb[:], ACT.Square)

        bj_words = held.tile([P, J], U16, name="bj_words", align_bytes=64)
        bj_scales = held.tile([P, J], U8, name="bj_scales", align_bytes=64)
        nc.vector.tensor_copy(bj_words[:], b_words[:].indirect(list_j[:]))
        nc.vector.tensor_copy(bj_scales[:], b_scales[:].indirect(list_j[:]))

        def gather_plane(woven, rows, t):
            nc.vector.tensor_copy(woven[:, :, t], rows[t].indirect(list_i[:]))

        def quantise(woven, name):
            codes = held.tile([P, I], U32, name=name + "_codes", align_bytes=64)
            scales = held.tile([P, I], U8, name=name + "_scales", align_bytes=64)
            nc.vector.quantize_mx(out=codes[:].bitcast(FP8X4), scales=scales[:], in_=woven[:].rearrange("p n t -> p (n t)"))
            return codes, scales

        a_woven = held.tile([P, I, PACK], BF16, name="a_woven", align_bytes=64)
        d_woven = held.tile([P, I, PACK], BF16, name="d_woven", align_bytes=64)
        a_pair = held.tile([P, 2, I], F32, name="a_pair")
        for t in (0, 1):
            nc.vector.tensor_copy(a_pair[:, t, :], a_rows[t].indirect(list_i[:]))
        nc.scalar.copy(a_woven[:, :, 0:2], a_pair[:].rearrange("p t n -> p n t"))
        for t in (2, 3):
            gather_plane(a_woven, a_rows, t)
        a_codes, a_scales = quantise(a_woven, "a")

        score = [[psum.tile([P, J_HALF], F32, name=f"score{h}{m}", tag=f"early{h}{m}") for m in range(I_TILES)] for h in range(HALVES)]
        scaled = [held.tile([P, I_TILES, J_HALF], F32, name=f"scaled{h}") for h in range(HALVES)]
        logit = [psum.tile([P, BLOCKS_PER_HALF, I], F32, name=f"logit{h}", tag=f"logit{h}") for h in range(HALVES)]
        for h in range(HALVES):
            js = slice(h * J_HALF, (h + 1) * J_HALF)
            for m in range(I_TILES):
                ms = slice(m * P, (m + 1) * P)
                nc.tensor.matmul_mx(out=score[h][m][:], lhsT=a_codes[:, ms].bitcast(FP8X4), lhsT_scale=a_scales[:, ms],
                                    rhs=bj_words[:, js].bitcast(FP4X4), rhs_scale=bj_scales[:, js], start=True, stop=True)
        half_bias = held.tile([P, J_BLOCKS], F32, name="half_bias")
        half_pw = held.tile([P, J_BLOCKS], F32, name="half_pw")
        neg_half_pw = held.tile([P, J_BLOCKS], F32, name="neg_half_pw")
        columns = psum.tile([P, P], F32, name="columns", tag="tangent0")
        nc.tensor.transpose(columns[:], vector_rows[:], identity[:])
        tanh = [held.tile([P, BLOCKS_PER_HALF, I], F32, name=f"tanh{h}") for h in range(HALVES)]
        for h in range(HALVES):
            for m in range(I_TILES):
                nc.scalar.activation(scaled[h][:, m, :], score[h][m][:], ACT.Copy, scale=steep_sb[:, m : m + 1])
            for b in range(BLOCKS_PER_HALF):
                for m in range(I_TILES):
                    nc.tensor.transpose(logit[h][:, b, m * P : (m + 1) * P], scaled[h][:, m, b * P : (b + 1) * P], identity[:])
        nc.scalar.activation(half_bias[:], columns[:, BIAS_AT : BIAS_AT + J_BLOCKS], ACT.Copy, scale=0.5)
        nc.scalar.activation(half_pw[:], columns[:, PW_AT : PW_AT + J_BLOCKS], ACT.Copy, scale=0.5)
        nc.scalar.activation(neg_half_pw[:], columns[:, PW_AT : PW_AT + J_BLOCKS], ACT.Copy, scale=-0.5)
        for t in range(PACK):
            gather_plane(d_woven, d_rows, t)
        d_codes, d_scales = quantise(d_woven, "d")
        degree_first = [psum.tile([P, I], F32, name=f"degree_first{b}", tag=f"early0{b}") for b in range(BLOCKS_PER_HALF)]
        degree_second = psum.tile([P, BLOCKS_PER_HALF, I], F32, name="degree_second", tag="early10")
        for h in range(HALVES):
            for b in range(BLOCKS_PER_HALF):
                target = degree_first[b][:] if h == 0 else degree_second[:, b, :]
                for m in range(I_TILES):
                    nc.tensor.transpose(target[:, m * P : (m + 1) * P], degree_sb[h][:, m, b * P : (b + 1) * P], identity[:])

        slope = [held.tile([P, BLOCKS_PER_HALF, I], F32, name=f"slope{h}") for h in range(HALVES)]
        poly = [held.tile([P, BLOCKS_PER_HALF, I], F32, name=f"poly{h}") for h in range(HALVES)]
        for h in range(HALVES):
            for b in range(BLOCKS_PER_HALF):
                col = h * BLOCKS_PER_HALF + b
                nc.scalar.activation(tanh[h][:, b, :], logit[h][:, b, :], ACT.Tanh, bias=half_bias[:, col : col + 1], scale=0.5)
        for h in range(HALVES):
            tanh_sq = held.tile([P, BLOCKS_PER_HALF, I], F32, name=f"tanh_sq{h}")
            nc.scalar.activation(tanh_sq[:], tanh[h][:], ACT.Square)
            for b in range(BLOCKS_PER_HALF):
                col = h * BLOCKS_PER_HALF + b
                nc.scalar.activation(slope[h][:, b, :], tanh_sq[:, b, :], ACT.Identity,
                                     bias=neg_half_pw[:, col : col + 1], scale=half_pw[:, col : col + 1])
        inner = [held.tile([P, BLOCKS_PER_HALF, I], F32, name=f"inner{h}") for h in range(HALVES)]
        for b in range(BLOCKS_PER_HALF):
            nc.vector.scalar_tensor_tensor(inner[0][:, b, :], tanh[0][:, b, :], 0.75, degree_first[b][:], ALU.mult, ALU.subtract)
        nc.vector.scalar_tensor_tensor(inner[1][:], tanh[1][:], 0.75, degree_second[:], ALU.mult, ALU.subtract)
        for h in range(HALVES):
            nc.vector.scalar_tensor_tensor(poly[h][:], inner[h][:], 0.5, tanh[h][:], ALU.add, ALU.mult)

        tangent = [psum.tile([P, BLOCKS_PER_HALF, I], F32, name=f"tangent{h}", tag=f"tangent{h}") for h in range(HALVES)]
        for h in range(HALVES):
            for b in range(BLOCKS_PER_HALF):
                js = slice(h * J_HALF + b * P, h * J_HALF + (b + 1) * P)
                nc.tensor.matmul_mx(out=tangent[h][:, b, :], lhsT=bj_words[:, js].bitcast(FP4X4), lhsT_scale=bj_scales[:, js],
                                    rhs=d_codes[:].bitcast(FP8X4), rhs_scale=d_scales[:], start=True, stop=True)
        factor = [held.tile([P, BLOCKS_PER_HALF, I], F32, name=f"factor{h}", tag=f"factor{h}") for h in range(HALVES)]
        change = [held.tile([P, BLOCKS_PER_HALF, I], F32, name=f"change{h}") for h in range(HALVES)]
        for h in range(HALVES):
            nc.vector.scalar_tensor_tensor(factor[h][:], poly[h][:], -0.25, slope[h][:], ALU.add, ALU.mult)
        for h in range(HALVES):
            nc.vector.tensor_tensor(change[h][:], tangent[h][:], factor[h][:], ALU.mult)
        out_by_tile = out.rearrange("(m p) j -> p m j", p=P)
        for h in range(HALVES):
            js = slice(h * J_HALF, (h + 1) * J_HALF)
            turned = [psum.tile([P, J_HALF], F32, name=f"turned{h}{m}", tag=TURNED_BANKS[h][m]) for m in range(I_TILES)]
            for m in range(I_TILES):
                for b in range(BLOCKS_PER_HALF):
                    nc.tensor.transpose(turned[m][:, b * P : (b + 1) * P], change[h][:, b, m * P : (m + 1) * P], identity[:])
            for m in range(I_TILES):
                result = held.tile([P, J_HALF], F32, name=f"result{h}{m}", tag=f"factor{HALVES - 1}" if h + m == 0 else f"result{h}{m}")
                nc.vector.scalar_tensor_tensor(result[:], turned[m][:], steep_sq[:, m : m + 1], base_sb[:, m, js], ALU.mult, ALU.add)
                nc.sync.dma_start(out_by_tile[:, m, js], result[:])
